import numpy as np
import ml_dtypes


def mxq(x, axis, fmt="e4m3"):
    dtype, down = {"e4m3": (ml_dtypes.float8_e4m3fn, 7), "e5m2": (ml_dtypes.float8_e5m2, 14)}[fmt]
    v = np.moveaxis(np.asarray(x, np.float32).astype(ml_dtypes.bfloat16).astype(np.float64), axis, -1)
    blocks = v.reshape(v.shape[:-1] + (-1, 32))
    amax = np.abs(blocks).max(-1, keepdims=True)
    byte = np.maximum(np.where(amax > 0, np.frexp(amax)[1] - 1 + 127, 0) - down, 1)
    scale = np.exp2(byte - 127.0)
    codes = (blocks / scale).astype(np.float32).astype(dtype).astype(np.float64)
    return np.moveaxis((codes * scale).reshape(v.shape), -1, axis)


WIDE = False


def mx_kscale(k):
    if not WIDE:
        return np.ones(k)
    levels = np.array([10, -10, 5, -5, 0])
    if k % 512:
        return np.exp2(np.random.permutation(np.resize(levels, k // 32))).repeat(32)
    a = np.empty((k // 512, 16))
    for p in range(k // 512):
        a[p, :8] = np.random.permutation(np.resize(levels, 8))
        for g in range(8):
            far = levels[np.abs(levels - a[p, g]) >= 10]
            a[p, g + 8] = far[np.random.randint(len(far))]
    return np.exp2(a.ravel()).repeat(32)


def f64(x):
    return np.asarray(x).astype(np.float64)


def striped(idx):
    return np.tile(idx.reshape(-1, 16).T, (8, 1)).astype(np.uint16)


def unstriped(offs):
    return offs[:16].T.reshape(-1).astype(np.int64)


def pack_weight(w):
    k, n = w.shape
    w = f64(np.asarray(w, np.float32).astype(ml_dtypes.bfloat16)).reshape(k // 32, 32, n)
    amax = np.abs(w).max(1)
    byte = np.clip(np.where(amax > 0, np.frexp(amax)[1] - 1 + 127 - 7, 1), 1, 254)
    scaled = (w * np.exp2(127.0 - byte)[:, None, :]).reshape(k, n).astype(np.float32)
    words = np.ascontiguousarray(scaled.reshape(k // 512, 128, 4, n).transpose(0, 1, 3, 2)).astype(ml_dtypes.float8_e4m3fn).view(np.uint8)
    return words, np.ascontiguousarray(byte.astype(np.uint8).reshape(k // 512, 16, n))


def unpack_weight(words, scales):
    g, p, n, _ = words.shape
    vals = np.ascontiguousarray(words).view(ml_dtypes.float8_e4m3fn).astype(np.float64) * np.repeat(np.exp2(scales.astype(np.float64) - 127.0), 8, axis=1)[..., None]
    return vals.transpose(0, 1, 3, 2).reshape(g * 512, n)


K, T, S, D, N, H, V, U = 512, 2048, 1024, 2, 128, 512, 512, 512


def setup_inputs():
    n = np.random.standard_normal
    s = mx_kscale(K)[:, None]
    u = mx_kscale(H)
    packed_xT = pack_weight(n((K, T)) * s)
    return {
        "x_words": packed_xT[0],
        "x_scales": packed_xT[1],
        "w1": (n((K, H)) / np.sqrt(K) / s).astype(np.float32),
        "w2": (n((K, H)) / np.sqrt(K) / s).astype(np.float32),
        "unit": (np.random.uniform(0.6, 1.4, (H, 1)) * u[:, None]).astype(np.float32),
        "w3": (n((H, N)) / np.sqrt(H) / u[:, None]).astype(np.float32),
        "offs": striped(np.random.permutation(T)[:S]),
        "s1": striped(np.random.randint(0, V, U)),
        "s2": striped(np.random.randint(0, V, U)),
    }


def reference(x_words, x_scales, w1, w2, unit, w3, offs, s1, s2):
    xq = unpack_weight(x_words, x_scales)[:, unstriped(offs)]
    re = mxq(f64(w1), 0, "e4m3").T @ xq
    im2 = mxq(f64(w2), 0, "e4m3").T @ xq
    pw = (re) ** 2 + (im2) ** 2
    p11 = pw.reshape(len(pw), -1, D).sum(axis=2) + 0.4
    pa1 = p11[:, unstriped(s1)]
    cx = re * (np.pad(re, ((0, 0), (0, 1)))[:, 1:]) + im2 * (np.pad(im2, ((0, 0), (0, 1)))[:, 1:])
    p12 = cx.reshape(len(cx), -1, D).sum(axis=2)
    pd1 = p12[:, unstriped(s1)]
    pa2 = p11[:, unstriped(s2)]
    spec = (pa1 - pd1) / (pa2 + 0.5)
    hid = f64(unit) * (np.log(np.abs(spec) + 0.2))
    return mxq(f64(w3), 0, "e4m3").T @ mxq(hid, 0, "e4m3")

@@ -1,0 +1,224 @@
+import math
+from contextlib import ExitStack
+
+import concourse.mybir as mybir
+from concourse.masks import make_identity
+
+K, T, S, H, V, N = 512, 2048, 1024, 512, 512, 128
+FLOPS = 2 * 2 * K * H * S + 2 * H * N * V
+
+F32 = mybir.dt.float32
+BF16 = mybir.dt.bfloat16
+I32 = mybir.dt.int32
+U32 = mybir.dt.uint32
+U16 = mybir.dt.uint16
+U8 = mybir.dt.uint8
+FP8X4 = mybir.dt.float8_e4m3fn_x4
+ALU = mybir.AluOpType
+ACT = mybir.ActivationFunctionType
+
+P = 128
+PACK = 4
+RUN = S // P
+PAIRS = RUN // 2
+CHUNK = 256
+LIST_ROWS = 16
+LAG = 2
+LAST_CHUNKS = ((0, 256), (256, 128), (384, 128))
+
+
+def tile_picked_ybeamfr_log_p_kernel(tc, x_words, x_scales, w1, w2, unit, w3, offs, s1, s2, out):
+    nc = tc.nc
+    with ExitStack() as ctx:
+        keep = ctx.enter_context(tc.tile_pool(name="keep", bufs=1))
+        terms = ctx.enter_context(tc.tile_pool(name="terms", bufs=4))
+        rows = ctx.enter_context(tc.tile_pool(name="rows", bufs=4))
+        small = ctx.enter_context(tc.tile_pool(name="small", bufs=4))
+        prod = ctx.enter_context(tc.psum_pool(name="prod", bufs=6))
+        sums = ctx.enter_context(tc.psum_pool(name="sums", bufs=1))
+
+        offs_t = keep.tile([P, S // LIST_ROWS], U16, name="offs_t")
+        s1_t = keep.tile([P, V // LIST_ROWS], U16, name="s1_t")
+        s2_t = keep.tile([P, V // LIST_ROWS], U16, name="s2_t")
+        xs_win = keep.tile([P, T], U8, name="xs_win", align_bytes=64)
+        xw_win = keep.tile([P, T], I32, name="xw_win", align_bytes=64)
+        w_raw = [keep.tile([P, PACK, H], F32, name=f"w_raw{c}") for c in range(2)]
+
+        nc.vector.memset(xs_win[:, 0 : 3 * T // 4].bitcast(I32), 0)
+        nc.gpsimd.memset(xs_win[:, 3 * T // 4 :].bitcast(I32), 0)
+        for q in range(4):
+            nc.scalar.dma_start(out=xs_win[32 * q : 32 * q + 4, :].bitcast(I32), in_=x_scales[0, 4 * q : 4 * q + 4, :].bitcast(I32))
+        nc.sync.dma_start(offs_t[:], offs)
+        nc.sync.dma_start(s2_t[:], s2)
+        nc.sync.dma_start(out=xw_win[:], in_=x_words[0].rearrange("p n r -> p (n r)").bitcast(I32))
+        nc.sync.dma_start(out=w_raw[0][:], in_=w1.rearrange("(p j) c -> p j c", j=PACK))
+        nc.sync.dma_start(s1_t[:], s1)
+        nc.sync.dma_start(out=w_raw[1][:], in_=w2.rearrange("(p j) c -> p j c", j=PACK))
+
+        ident = keep.tile([P, P], F32, name="ident")
+        make_identity(nc, ident[:])
+
+        got_s = keep.tile([P, S + RUN], U8, name="got_s", align_bytes=64)
+        got_w = keep.tile([P, S + RUN], I32, name="got_w", align_bytes=64)
+        nc.vector.memset(got_s[:, S:].bitcast(I32), 0)
+        nc.vector.memset(got_w[:, S:], 0)
+        x_s = keep.tile([P, RUN + 1, P], U8, name="x_s", align_bytes=64)
+        x_w = keep.tile([P, RUN + 1, P], I32, name="x_w", align_bytes=64)
+
+        def deal(dealt, got):
+            nc.vector.tensor_copy(
+                out=dealt[:, 0:RUN, :].rearrange("k (u m) p -> k u p m", u=2),
+                in_=got[:, 0:S].rearrange("k (p u m) -> k u p m", u=2, m=RUN // 2),
+            )
+            nc.vector.tensor_copy(out=dealt[:, RUN, :], in_=got[:, RUN : S + RUN : RUN])
+
+        w_bf = [keep.tile([P, PACK, P, PACK], BF16, name=f"w_bf{c}", align_bytes=64) for c in range(2)]
+        w_w = [keep.tile([P, H], U32, name=f"w_w{c}", align_bytes=64) for c in range(2)]
+        w_s = [keep.tile([P, H], U8, name=f"w_s{c}", align_bytes=64) for c in range(2)]
+
+        def cast_w(c):
+            nc.scalar.copy(
+                out=w_bf[c][:].rearrange("p t m j -> p m j t"),
+                in_=w_raw[c][:].rearrange("p j (m t) -> p m j t", t=PACK),
+            )
+
+        def quant_w(c):
+            for t in range(PACK):
+                cols = slice(t * P, (t + 1) * P)
+                nc.vector.quantize_mx(out=w_w[c][:, cols].bitcast(FP8X4), scales=w_s[c][:, cols], in_=w_bf[c][:, t, :, :].rearrange("p m j -> p (m j)"))
+
+        nc.vector.tensor_copy(out=got_s[:, 0:S], in_=xs_win[:].indirect(offs_t[:]))
+        nc.vector.tensor_copy(out=got_w[:, 0:S].bitcast(U32), in_=xw_win[:].bitcast(U32).indirect(offs_t[:]))
+        deal(x_s[:], got_s[:])
+        deal(x_w[:].bitcast(U32), got_w[:].bitcast(U32))
+        cast_w(0)
+        quant_w(0)
+        cast_w(1)
+        quant_w(1)
+        w3_raw = keep.tile([P, PACK, N], F32, name="w_raw0")
+        unit_t = keep.tile([P, PACK], F32, name="w_raw1")
+        nc.sync.dma_start(out=w3_raw[:], in_=w3.rearrange("(p j) n -> p j n", j=PACK))
+        nc.sync.dma_start(out=unit_t[:], in_=unit.rearrange("(p t) o -> p (t o)", t=PACK))
+
+        def product(bank, m, c, cols):
+            nc.tensor.matmul_mx(
+                out=bank,
+                lhsT=x_w[:, m, :].bitcast(FP8X4),
+                lhsT_scale=x_s[:, m, :],
+                rhs=w_w[c][:, cols].bitcast(FP8X4),
+                rhs_scale=w_s[c][:, cols],
+                start=True,
+                stop=True,
+            )
+
+        even = [keep.tile([P, PACK, PAIRS + 1, P], F32, name=f"even{c}") for c in range(2)]
+
+        def last_even(c):
+            bank = prod.tile([P, H], F32, name="bank")
+            product(bank[:], RUN, c, slice(0, H))
+            nc.scalar.copy(out=even[c][:, :, PAIRS, :], in_=bank[:].rearrange("v (t i) -> v t i", t=PACK))
+
+        def make_terms(t, c):
+            cols = slice(t * P, (t + 1) * P)
+            bank_a = prod.tile([P, PAIRS * P], F32, name="bank")
+            for h in range(PAIRS):
+                product(bank_a[:, h * P : (h + 1) * P], 2 * h, c, cols)
+            bank_b = prod.tile([P, PAIRS * P], F32, name="bank")
+            for h in range(PAIRS):
+                product(bank_b[:, h * P : (h + 1) * P], 2 * h + 1, c, cols)
+            a_all = even[c][:, t, :, :].rearrange("v h i -> v (h i)")
+            a = a_all[:, 0 : PAIRS * P]
+            nc.vector.tensor_copy(out=a, in_=bank_a[:])
+            sq_b = terms.tile([P, PAIRS * P], F32, name="sq_b")
+            nc.scalar.activation(out=sq_b[:], in_=bank_b[:], func=ACT.Square)
+            both = terms.tile([P, PAIRS * P], F32, name="both")
+            nc.vector.tensor_tensor(out=both[:], in0=a, in1=a_all[:, P:], op=ALU.add)
+            sq_a = terms.tile([P, PAIRS * P], F32, name="sq_a")
+            nc.scalar.activation(out=sq_a[:], in_=a, func=ACT.Square)
+            cross = terms.tile([P, PAIRS * P], F32, name="cross")
+            nc.vector.tensor_tensor(out=cross[:], in0=bank_b[:], in1=both[:], op=ALU.mult)
+            return sq_b, sq_a, cross
+
+        def add_turned(bank, parts, first, last):
+            for n, part in enumerate(parts):
+                for h in range(PAIRS):
+                    cols = slice(h * P, (h + 1) * P)
+                    nc.tensor.matmul(
+                        bank[:, cols], lhsT=part[:, cols], rhs=ident[:], is_transpose=True,
+                        start=first and n == 0 and h == 0,
+                        stop=last and n == len(parts) - 1 and h == PAIRS - 1,
+                    )
+
+        hid = keep.tile([P, PACK - 1, V], BF16, name="hid", align_bytes=64)
+        woven = keep.tile([P, V, PACK], BF16, name="woven", align_bytes=64)
+
+        def windows(re_terms, im_terms):
+            power = sums.tile([P, V], F32, name="power")
+            corr = sums.tile([P, V], F32, name="corr")
+            add_turned(power, re_terms[:2], True, False)
+            add_turned(corr, re_terms[2:], True, False)
+            add_turned(power, im_terms[:2], False, True)
+            add_turned(corr, im_terms[2:], False, True)
+            den = rows.tile([P, V], F32, name="den")
+            den_v = den[:].rearrange("i (p h) -> i p h", h=PAIRS)
+            nc.scalar.activation(out=den_v, in_=power[:].rearrange("i (h p) -> i p h", h=PAIRS), func=ACT.Copy, bias=0.9)
+            signed = small.tile([P, V], F32, name="signed")
+            nc.vector.scalar_tensor_tensor(
+                out=signed[:].rearrange("i (p h) -> i p h", h=PAIRS), in0=corr[:].rearrange("i (h p) -> i p h", h=PAIRS), scalar=0.5,
+                in1=den_v, op0=ALU.add, op1=ALU.subtract,
+            )
+            num = rows.tile([P, V], F32, name="num")
+            nc.scalar.activation(out=num[:], in_=signed[:], func=ACT.Abs, scale=5.0)
+            return den, num
+
+        def hidden(t, den, num, v0, width):
+            lst = slice(v0 // LIST_ROWS, (v0 + width) // LIST_ROWS)
+            cols = slice(v0, v0 + width)
+            args = small.tile([P, 2, width], F32, name="args")
+            nc.scalar.activation(out=args[:, 0, :], in_=den[:].indirect(s2_t[:, lst]), func=ACT.Copy)
+            nc.vector.tensor_tensor(out=args[:, 1, :], in0=num[:].indirect(s1_t[:, lst]), in1=args[:, 0, :], op=ALU.add)
+            logs = small.tile([P, 2, width], F32, name="logs")
+            nc.scalar.activation(out=logs[:], in_=args[:], func=ACT.Ln)
+            diff = small.tile([P, width], F32, name="diff")
+            nc.vector.scalar_tensor_tensor(out=diff[:], in0=logs[:, 1, :], scalar=-math.log(5.0), in1=logs[:, 0, :], op0=ALU.add, op1=ALU.subtract)
+            target = woven[:, cols, t] if t == PACK - 1 else hid[:, t, cols]
+            nc.vector.tensor_scalar(out=target, in0=diff[:], scalar1=unit_t[:, t : t + 1], scalar2=None, op0=ALU.mult)
+            if t == PACK - 2:
+                nc.vector.tensor_copy(out=woven[:, cols, 0 : PACK - 1], in_=hid[:, :, cols].rearrange("p t v -> p v t"))
+
+        w3_bf = keep.tile([P, N, PACK], BF16, name="w3_bf", align_bytes=64)
+        w3_w = keep.tile([P, N], U32, name="w3_w", align_bytes=64)
+        w3_s = keep.tile([P, N], U8, name="w3_s", align_bytes=64)
+
+        def features(v0, width):
+            hid_w = small.tile([P, width], U32, name="hid_w", align_bytes=64)
+            hid_s = small.tile([P, width], U8, name="hid_s", align_bytes=64)
+            nc.vector.quantize_mx(out=hid_w[:].bitcast(FP8X4), scales=hid_s[:], in_=woven[:, v0 : v0 + width, :].rearrange("p v t -> p (v t)"))
+            bank = prod.tile([P, width], F32, name="bank")
+            nc.tensor.matmul_mx(
+                out=bank[:], lhsT=w3_w[:].bitcast(FP8X4), lhsT_scale=w3_s[:], rhs=hid_w[:].bitcast(FP8X4), rhs_scale=hid_s[:],
+                start=True, stop=True,
+            )
+            result = small.tile([P, width], F32, name="result")
+            nc.scalar.copy(out=result[:], in_=bank[:])
+            nc.sync.dma_start(out=out[:, v0 : v0 + width], in_=result[:])
+
+        last_even(0)
+        wins = []
+        for t in range(PACK):
+            re_terms = make_terms(t, 0)
+            if t == 0:
+                last_even(1)
+            im_terms = make_terms(t, 1)
+            if t >= LAG:
+                for v0 in range(0, V, CHUNK):
+                    hidden(t - LAG, *wins[t - LAG], v0, CHUNK)
+            wins.append(windows(re_terms, im_terms))
+        nc.scalar.copy(out=w3_bf[:], in_=w3_raw[:].rearrange("p j n -> p n j"))
+        nc.vector.quantize_mx(out=w3_w[:].bitcast(FP8X4), scales=w3_s[:], in_=w3_bf[:].rearrange("p n j -> p (n j)"))
+        for t in range(PACK - LAG, PACK - 1):
+            for v0 in range(0, V, CHUNK):
+                hidden(t, *wins[t], v0, CHUNK)
+        for v0, width in LAST_CHUNKS:
+            hidden(PACK - 1, *wins[PACK - 1], v0, width)
+            features(v0, width)

@@ -1,4 +1,3 @@
-import math
 from contextlib import ExitStack
 
 import concourse.mybir as mybir
@@ -24,7 +23,7 @@ PAIRS = RUN // 2
 CHUNK = 256
 LIST_ROWS = 16
 LAG = 2
-LAST_CHUNKS = ((0, 256), (256, 128), (384, 128))
+SPARE = 32
 
 
 def tile_picked_ybeamfr_log_p_kernel(tc, x_words, x_scales, w1, w2, unit, w3, offs, s1, s2, out):
@@ -32,7 +31,6 @@ def tile_picked_ybeamfr_log_p_kernel(tc, x_words, x_scales, w1, w2, unit, w3, of
     with ExitStack() as ctx:
         keep = ctx.enter_context(tc.tile_pool(name="keep", bufs=1))
         terms = ctx.enter_context(tc.tile_pool(name="terms", bufs=4))
-        rows = ctx.enter_context(tc.tile_pool(name="rows", bufs=4))
         small = ctx.enter_context(tc.tile_pool(name="small", bufs=4))
         prod = ctx.enter_context(tc.psum_pool(name="prod", bufs=6))
         sums = ctx.enter_context(tc.psum_pool(name="sums", bufs=1))
@@ -41,26 +39,37 @@ def tile_picked_ybeamfr_log_p_kernel(tc, x_words, x_scales, w1, w2, unit, w3, of
         s1_t = keep.tile([P, V // LIST_ROWS], U16, name="s1_t")
         s2_t = keep.tile([P, V // LIST_ROWS], U16, name="s2_t")
         xs_win = keep.tile([P, T], U8, name="xs_win", align_bytes=64)
-        xw_win = keep.tile([P, T], I32, name="xw_win", align_bytes=64)
-        w_raw = [keep.tile([P, PACK, H], F32, name=f"w_raw{c}") for c in range(2)]
-
+        one = keep.tile([P, 1], F32, name="xw_win", align_bytes=64)
+        nc.gpsimd.memset(one[:], 1.0)
         nc.vector.memset(xs_win[:, 0 : 3 * T // 4].bitcast(I32), 0)
         nc.gpsimd.memset(xs_win[:, 3 * T // 4 :].bitcast(I32), 0)
-        for q in range(4):
-            nc.scalar.dma_start(out=xs_win[32 * q : 32 * q + 4, :].bitcast(I32), in_=x_scales[0, 4 * q : 4 * q + 4, :].bitcast(I32))
+        fifth = keep.tile([P, 1], F32, name="w1_raw")
+        nc.vector.tensor_scalar(out=fifth[:], in0=one[:], scalar1=0.2, scalar2=None, op0=ALU.mult)
+        ln_fifth = keep.tile([P, 1], F32, name="ln_fifth")
+        nc.scalar.activation(out=ln_fifth[:], in_=fifth[:], func=ACT.Ln)
+
         nc.sync.dma_start(offs_t[:], offs)
         nc.sync.dma_start(s2_t[:], s2)
-        nc.sync.dma_start(out=xw_win[:], in_=x_words[0].rearrange("p n r -> p (n r)").bitcast(I32))
-        nc.sync.dma_start(out=w_raw[0][:], in_=w1.rearrange("(p j) c -> p j c", j=PACK))
         nc.sync.dma_start(s1_t[:], s1)
-        nc.sync.dma_start(out=w_raw[1][:], in_=w2.rearrange("(p j) c -> p j c", j=PACK))
+        for q in range(4):
+            queue = nc.sync if q < 2 else nc.scalar
+            queue.dma_start(out=xs_win[32 * q : 32 * q + 4, :].bitcast(I32), in_=x_scales[0, 4 * q : 4 * q + 4, :].bitcast(I32))
+        xw_win = keep.tile([P, T], I32, name="xw_win", align_bytes=64)
+        nc.sync.dma_start(out=xw_win[:], in_=x_words[0].rearrange("p n r -> p (n r)").bitcast(I32))
+        w1_raw = keep.tile([P, PACK, H], F32, name="w1_raw")
+        nc.sync.dma_start(out=w1_raw[:], in_=w1.rearrange("(p j) c -> p j c", j=PACK))
+
+        den = [keep.tile([P, V + SPARE], F32, name=f"den{t}") for t in range(PACK)]
+        num = [keep.tile([P, V + SPARE], F32, name=f"num{t}") for t in range(PACK)]
 
         ident = keep.tile([P, P], F32, name="ident")
         make_identity(nc, ident[:])
+        for window in den + num:
+            nc.gpsimd.memset(window[:, V:], 0.0)
 
         got_s = keep.tile([P, S + RUN], U8, name="got_s", align_bytes=64)
-        got_w = keep.tile([P, S + RUN], I32, name="got_w", align_bytes=64)
         nc.vector.memset(got_s[:, S:].bitcast(I32), 0)
+        got_w = keep.tile([P, S + RUN], I32, name="got_w", align_bytes=64)
         nc.vector.memset(got_w[:, S:], 0)
         x_s = keep.tile([P, RUN + 1, P], U8, name="x_s", align_bytes=64)
         x_w = keep.tile([P, RUN + 1, P], I32, name="x_w", align_bytes=64)
@@ -76,27 +85,26 @@ def tile_picked_ybeamfr_log_p_kernel(tc, x_words, x_scales, w1, w2, unit, w3, of
         w_w = [keep.tile([P, H], U32, name=f"w_w{c}", align_bytes=64) for c in range(2)]
         w_s = [keep.tile([P, H], U8, name=f"w_s{c}", align_bytes=64) for c in range(2)]
 
-        def cast_w(c):
-            nc.scalar.copy(
-                out=w_bf[c][:].rearrange("p t m j -> p m j t"),
-                in_=w_raw[c][:].rearrange("p j (m t) -> p m j t", t=PACK),
-            )
-
-        def quant_w(c):
-            for t in range(PACK):
-                cols = slice(t * P, (t + 1) * P)
-                nc.vector.quantize_mx(out=w_w[c][:, cols].bitcast(FP8X4), scales=w_s[c][:, cols], in_=w_bf[c][:, t, :, :].rearrange("p m j -> p (m j)"))
+        def quantise_weight(c, raw):
+            for t0 in range(0, PACK, 2):
+                slots = slice(t0, t0 + 2)
+                cols = slice(t0 * P, (t0 + 2) * P)
+                nc.scalar.copy(
+                    out=w_bf[c][:, slots, :, :].rearrange("p t m j -> p m j t"),
+                    in_=raw[:].rearrange("p j (m t) -> p m j t", t=PACK)[:, :, :, slots],
+                )
+                nc.vector.quantize_mx(out=w_w[c][:, cols].bitcast(FP8X4), scales=w_s[c][:, cols], in_=w_bf[c][:, slots, :, :].rearrange("p t m j -> p (t m j)"))
 
         nc.vector.tensor_copy(out=got_s[:, 0:S], in_=xs_win[:].indirect(offs_t[:]))
-        nc.vector.tensor_copy(out=got_w[:, 0:S].bitcast(U32), in_=xw_win[:].bitcast(U32).indirect(offs_t[:]))
+        w2_raw = keep.tile([P, PACK, H], F32, name="xs_win", align_bytes=64)
+        nc.sync.dma_start(out=w2_raw[:], in_=w2.rearrange("(p j) c -> p j c", j=PACK))
         deal(x_s[:], got_s[:])
+        nc.vector.tensor_copy(out=got_w[:, 0:S].bitcast(U32), in_=xw_win[:].bitcast(U32).indirect(offs_t[:]))
         deal(x_w[:].bitcast(U32), got_w[:].bitcast(U32))
-        cast_w(0)
-        quant_w(0)
-        cast_w(1)
-        quant_w(1)
-        w3_raw = keep.tile([P, PACK, N], F32, name="w_raw0")
-        unit_t = keep.tile([P, PACK], F32, name="w_raw1")
+        quantise_weight(0, w1_raw)
+        quantise_weight(1, w2_raw)
+        w3_raw = keep.tile([P, PACK, N], F32, name="w1_raw")
+        unit_t = keep.tile([P, PACK], F32, name="xw_win", align_bytes=64)
         nc.sync.dma_start(out=w3_raw[:], in_=w3.rearrange("(p j) n -> p j n", j=PACK))
         nc.sync.dma_start(out=unit_t[:], in_=unit.rearrange("(p t) o -> p (t o)", t=PACK))
 
@@ -128,7 +136,10 @@ def tile_picked_ybeamfr_log_p_kernel(tc, x_words, x_scales, w1, w2, unit, w3, of
                 product(bank_b[:, h * P : (h + 1) * P], 2 * h + 1, c, cols)
             a_all = even[c][:, t, :, :].rearrange("v h i -> v (h i)")
             a = a_all[:, 0 : PAIRS * P]
-            nc.vector.tensor_copy(out=a, in_=bank_a[:])
+            if c == 0:
+                nc.vector.tensor_copy(out=a, in_=bank_a[:])
+            else:
+                nc.scalar.copy(out=a, in_=bank_a[:])
             sq_b = terms.tile([P, PAIRS * P], F32, name="sq_b")
             nc.scalar.activation(out=sq_b[:], in_=bank_b[:], func=ACT.Square)
             both = terms.tile([P, PAIRS * P], F32, name="both")
@@ -152,35 +163,32 @@ def tile_picked_ybeamfr_log_p_kernel(tc, x_words, x_scales, w1, w2, unit, w3, of
         hid = keep.tile([P, PACK - 1, V], BF16, name="hid", align_bytes=64)
         woven = keep.tile([P, V, PACK], BF16, name="woven", align_bytes=64)
 
-        def windows(re_terms, im_terms):
+        def windows(t, re_terms, im_terms):
             power = sums.tile([P, V], F32, name="power")
             corr = sums.tile([P, V], F32, name="corr")
             add_turned(power, re_terms[:2], True, False)
             add_turned(corr, re_terms[2:], True, False)
             add_turned(power, im_terms[:2], False, True)
             add_turned(corr, im_terms[2:], False, True)
-            den = rows.tile([P, V], F32, name="den")
-            den_v = den[:].rearrange("i (p h) -> i p h", h=PAIRS)
-            nc.scalar.activation(out=den_v, in_=power[:].rearrange("i (h p) -> i p h", h=PAIRS), func=ACT.Copy, bias=0.9)
+            den_v = den[t][:, 0:V].rearrange("i (p h) -> i p h", h=PAIRS)
+            nc.vector.tensor_scalar(out=den_v, in0=power[:].rearrange("i (h p) -> i p h", h=PAIRS), scalar1=0.9, scalar2=None, op0=ALU.add)
             signed = small.tile([P, V], F32, name="signed")
             nc.vector.scalar_tensor_tensor(
                 out=signed[:].rearrange("i (p h) -> i p h", h=PAIRS), in0=corr[:].rearrange("i (h p) -> i p h", h=PAIRS), scalar=0.5,
                 in1=den_v, op0=ALU.add, op1=ALU.subtract,
             )
-            num = rows.tile([P, V], F32, name="num")
-            nc.scalar.activation(out=num[:], in_=signed[:], func=ACT.Abs, scale=5.0)
-            return den, num
+            nc.scalar.activation(out=num[t][:, 0:V], in_=signed[:], func=ACT.Abs, scale=5.0)
 
-        def hidden(t, den, num, v0, width):
+        def hidden(t, v0, width):
             lst = slice(v0 // LIST_ROWS, (v0 + width) // LIST_ROWS)
             cols = slice(v0, v0 + width)
             args = small.tile([P, 2, width], F32, name="args")
-            nc.scalar.activation(out=args[:, 0, :], in_=den[:].indirect(s2_t[:, lst]), func=ACT.Copy)
-            nc.vector.tensor_tensor(out=args[:, 1, :], in0=num[:].indirect(s1_t[:, lst]), in1=args[:, 0, :], op=ALU.add)
+            nc.scalar.activation(out=args[:, 0, :], in_=den[t][:].indirect(s2_t[:, lst]), func=ACT.Copy)
+            nc.vector.tensor_tensor(out=args[:, 1, :], in0=num[t][:].indirect(s1_t[:, lst]), in1=args[:, 0, :], op=ALU.add)
             logs = small.tile([P, 2, width], F32, name="logs")
             nc.scalar.activation(out=logs[:], in_=args[:], func=ACT.Ln)
             diff = small.tile([P, width], F32, name="diff")
-            nc.vector.scalar_tensor_tensor(out=diff[:], in0=logs[:, 1, :], scalar=-math.log(5.0), in1=logs[:, 0, :], op0=ALU.add, op1=ALU.subtract)
+            nc.vector.scalar_tensor_tensor(out=diff[:], in0=logs[:, 1, :], scalar=ln_fifth[:], in1=logs[:, 0, :], op0=ALU.add, op1=ALU.subtract)
             target = woven[:, cols, t] if t == PACK - 1 else hid[:, t, cols]
             nc.vector.tensor_scalar(out=target, in0=diff[:], scalar1=unit_t[:, t : t + 1], scalar2=None, op0=ALU.mult)
             if t == PACK - 2:
@@ -204,21 +212,18 @@ def tile_picked_ybeamfr_log_p_kernel(tc, x_words, x_scales, w1, w2, unit, w3, of
             nc.sync.dma_start(out=out[:, v0 : v0 + width], in_=result[:])
 
         last_even(0)
-        wins = []
         for t in range(PACK):
             re_terms = make_terms(t, 0)
             if t == 0:
                 last_even(1)
             im_terms = make_terms(t, 1)
+            windows(t, re_terms, im_terms)
             if t >= LAG:
-                for v0 in range(0, V, CHUNK):
-                    hidden(t - LAG, *wins[t - LAG], v0, CHUNK)
-            wins.append(windows(re_terms, im_terms))
+                hidden(t - LAG, 0, V)
         nc.scalar.copy(out=w3_bf[:], in_=w3_raw[:].rearrange("p j n -> p n j"))
         nc.vector.quantize_mx(out=w3_w[:].bitcast(FP8X4), scales=w3_s[:], in_=w3_bf[:].rearrange("p n j -> p (n j)"))
         for t in range(PACK - LAG, PACK - 1):
-            for v0 in range(0, V, CHUNK):
-                hidden(t, *wins[t], v0, CHUNK)
-        for v0, width in LAST_CHUNKS:
-            hidden(PACK - 1, *wins[PACK - 1], v0, width)
-            features(v0, width)
+            hidden(t, 0, V)
+        for v0 in range(0, V, CHUNK):
+            hidden(PACK - 1, v0, CHUNK)
+            features(v0, CHUNK)

@@ -24,6 +24,9 @@ CHUNK = 256
 LIST_ROWS = 16
 LAG = 2
 SPARE = 32
+PLAIN = 2
+TURNED = PACK - PLAIN
+HALF = S // 2
 
 
 def tile_picked_ybeamfr_log_p_kernel(tc, x_words, x_scales, w1, w2, unit, w3, offs, s1, s2, out):
@@ -64,7 +67,8 @@ def tile_picked_ybeamfr_log_p_kernel(tc, x_words, x_scales, w1, w2, unit, w3, of
 
         ident = keep.tile([P, P], F32, name="ident")
         make_identity(nc, ident[:])
-        for window in den + num:
+        firsts = [[keep.tile([P, V + 8], F32, name=f"firsts{t}{c}") for c in range(2)] for t in range(PLAIN)]
+        for window in den + num + sum(firsts, []):
             nc.gpsimd.memset(window[:, V:], 0.0)
 
         got_s = keep.tile([P, S + RUN], U8, name="got_s", align_bytes=64)
@@ -98,9 +102,7 @@ def tile_picked_ybeamfr_log_p_kernel(tc, x_words, x_scales, w1, w2, unit, w3, of
         nc.vector.tensor_copy(out=got_s[:, 0:S], in_=xs_win[:].indirect(offs_t[:]))
         w2_raw = keep.tile([P, PACK, H], F32, name="xs_win", align_bytes=64)
         nc.sync.dma_start(out=w2_raw[:], in_=w2.rearrange("(p j) c -> p j c", j=PACK))
-        deal(x_s[:], got_s[:])
         nc.vector.tensor_copy(out=got_w[:, 0:S].bitcast(U32), in_=xw_win[:].bitcast(U32).indirect(offs_t[:]))
-        deal(x_w[:].bitcast(U32), got_w[:].bitcast(U32))
         quantise_weight(0, w1_raw)
         quantise_weight(1, w2_raw)
         w3_raw = keep.tile([P, PACK, N], F32, name="w1_raw")
@@ -119,12 +121,50 @@ def tile_picked_ybeamfr_log_p_kernel(tc, x_words, x_scales, w1, w2, unit, w3, of
                 stop=True,
             )
 
-        even = [keep.tile([P, PACK, PAIRS + 1, P], F32, name=f"even{c}") for c in range(2)]
+        even = [keep.tile([P, TURNED, PAIRS + 1, P], F32, name=f"even{c}") for c in range(2)]
 
         def last_even(c):
-            bank = prod.tile([P, H], F32, name="bank")
-            product(bank[:], RUN, c, slice(0, H))
-            nc.scalar.copy(out=even[c][:, :, PAIRS, :], in_=bank[:].rearrange("v (t i) -> v t i", t=PACK))
+            bank = sums.tile([P, TURNED * P], F32, name=("power", "corr")[c])
+            product(bank[:], RUN, c, slice(PLAIN * P, H))
+            nc.scalar.copy(out=even[c][:, :, PAIRS, :], in_=bank[:].rearrange("v (t i) -> v t i", t=TURNED))
+
+        def plain_terms(t, c):
+            cols = slice(t * P, (t + 1) * P)
+            a = firsts[t][c]
+            squares = terms.tile([P, 2, V], F32, name="squares")
+            banks = []
+            for u in range(2):
+                entries = slice(u * HALF, (u + 1) * HALF)
+                vs = slice(u * CHUNK, (u + 1) * CHUNK)
+                bank = prod.tile([P, HALF], F32, name="bank")
+                nc.tensor.matmul_mx(
+                    out=bank[:], lhsT=w_w[c][:, cols].bitcast(FP8X4), lhsT_scale=w_s[c][:, cols],
+                    rhs=got_w[:, entries].bitcast(FP8X4), rhs_scale=got_s[:, entries], start=True, stop=True,
+                )
+                by_member = bank[:].rearrange("i (v d) -> i d v", d=2)
+                if t == 0:
+                    nc.vector.tensor_copy(out=a[:, vs], in_=by_member[:, 0, :])
+                else:
+                    nc.scalar.copy(out=a[:, vs], in_=by_member[:, 0, :])
+                nc.scalar.activation(out=squares[:, :, vs], in_=by_member, func=ACT.Square)
+                banks.append(by_member)
+            both = terms.tile([P, V], F32, name="both")
+            nc.vector.tensor_tensor(out=both[:], in0=a[:, 0:V], in1=a[:, 1 : V + 1], op=ALU.add)
+            cross = terms.tile([P, V], F32, name="cross")
+            for u in range(2):
+                vs = slice(u * CHUNK, (u + 1) * CHUNK)
+                nc.vector.tensor_tensor(out=cross[:, vs], in0=banks[u][:, 1, :], in1=both[:, vs], op=ALU.mult)
+            return squares, cross
+
+        def plain_windows(t, re_terms, im_terms):
+            power = small.tile([P, 2, V], F32, name="power2")
+            nc.vector.tensor_tensor(out=power[:], in0=re_terms[0][:], in1=im_terms[0][:], op=ALU.add)
+            nc.vector.scalar_tensor_tensor(out=den[t][:, 0:V], in0=power[:, 0, :], scalar=0.9, in1=power[:, 1, :], op0=ALU.add, op1=ALU.add)
+            partial = small.tile([P, V], F32, name="partial")
+            nc.vector.scalar_tensor_tensor(out=partial[:], in0=re_terms[1][:], scalar=0.5, in1=den[t][:, 0:V], op0=ALU.add, op1=ALU.subtract)
+            signed = small.tile([P, V], F32, name="signed")
+            nc.vector.tensor_tensor(out=signed[:], in0=partial[:], in1=im_terms[1][:], op=ALU.add)
+            nc.scalar.activation(out=num[t][:, 0:V], in_=signed[:], func=ACT.Abs, scale=5.0)
 
         def make_terms(t, c):
             cols = slice(t * P, (t + 1) * P)
@@ -134,12 +174,9 @@ def tile_picked_ybeamfr_log_p_kernel(tc, x_words, x_scales, w1, w2, unit, w3, of
             bank_b = prod.tile([P, PAIRS * P], F32, name="bank")
             for h in range(PAIRS):
                 product(bank_b[:, h * P : (h + 1) * P], 2 * h + 1, c, cols)
-            a_all = even[c][:, t, :, :].rearrange("v h i -> v (h i)")
+            a_all = even[c][:, t - PLAIN, :, :].rearrange("v h i -> v (h i)")
             a = a_all[:, 0 : PAIRS * P]
-            if c == 0:
-                nc.vector.tensor_copy(out=a, in_=bank_a[:])
-            else:
-                nc.scalar.copy(out=a, in_=bank_a[:])
+            nc.scalar.copy(out=a, in_=bank_a[:])
             sq_b = terms.tile([P, PAIRS * P], F32, name="sq_b")
             nc.scalar.activation(out=sq_b[:], in_=bank_b[:], func=ACT.Square)
             both = terms.tile([P, PAIRS * P], F32, name="both")
@@ -211,13 +248,16 @@ def tile_picked_ybeamfr_log_p_kernel(tc, x_words, x_scales, w1, w2, unit, w3, of
             nc.scalar.copy(out=result[:], in_=bank[:])
             nc.sync.dma_start(out=out[:, v0 : v0 + width], in_=result[:])
 
-        last_even(0)
         for t in range(PACK):
-            re_terms = make_terms(t, 0)
-            if t == 0:
-                last_even(1)
-            im_terms = make_terms(t, 1)
-            windows(t, re_terms, im_terms)
+            if t < PLAIN:
+                plain_windows(t, plain_terms(t, 0), plain_terms(t, 1))
+            else:
+                if t == PLAIN:
+                    deal(x_s[:], got_s[:])
+                    deal(x_w[:].bitcast(U32), got_w[:].bitcast(U32))
+                    last_even(0)
+                    last_even(1)
+                windows(t, make_terms(t, 0), make_terms(t, 1))
             if t >= LAG:
                 hidden(t - LAG, 0, V)
         nc.scalar.copy(out=w3_bf[:], in_=w3_raw[:].rearrange("p j n -> p n j"))

@@ -46,7 +46,7 @@ def tile_picked_ybeamfr_log_p_kernel(tc, x_words, x_scales, w1, w2, unit, w3, of
         nc.gpsimd.memset(one[:], 1.0)
         nc.vector.memset(xs_win[:, 0 : 3 * T // 4].bitcast(I32), 0)
         nc.gpsimd.memset(xs_win[:, 3 * T // 4 :].bitcast(I32), 0)
-        fifth = keep.tile([P, 1], F32, name="w1_raw")
+        fifth = keep.tile([P, 1], F32, name="w1_raw", align_bytes=64)
         nc.vector.tensor_scalar(out=fifth[:], in0=one[:], scalar1=0.2, scalar2=None, op0=ALU.mult)
         ln_fifth = keep.tile([P, 1], F32, name="ln_fifth")
         nc.scalar.activation(out=ln_fifth[:], in_=fifth[:], func=ACT.Ln)
@@ -59,7 +59,7 @@ def tile_picked_ybeamfr_log_p_kernel(tc, x_words, x_scales, w1, w2, unit, w3, of
             queue.dma_start(out=xs_win[32 * q : 32 * q + 4, :].bitcast(I32), in_=x_scales[0, 4 * q : 4 * q + 4, :].bitcast(I32))
         xw_win = keep.tile([P, T], I32, name="xw_win", align_bytes=64)
         nc.sync.dma_start(out=xw_win[:], in_=x_words[0].rearrange("p n r -> p (n r)").bitcast(I32))
-        w1_raw = keep.tile([P, PACK, H], F32, name="w1_raw")
+        w1_raw = keep.tile([P, PACK, H], F32, name="w1_raw", align_bytes=64)
         nc.sync.dma_start(out=w1_raw[:], in_=w1.rearrange("(p j) c -> p j c", j=PACK))
 
         den = [keep.tile([P, V + SPARE], F32, name=f"den{t}") for t in range(PACK)]
@@ -75,8 +75,6 @@ def tile_picked_ybeamfr_log_p_kernel(tc, x_words, x_scales, w1, w2, unit, w3, of
         nc.vector.memset(got_s[:, S:].bitcast(I32), 0)
         got_w = keep.tile([P, S + RUN], I32, name="got_w", align_bytes=64)
         nc.vector.memset(got_w[:, S:], 0)
-        x_s = keep.tile([P, RUN + 1, P], U8, name="x_s", align_bytes=64)
-        x_w = keep.tile([P, RUN + 1, P], I32, name="x_w", align_bytes=64)
 
         def deal(dealt, got):
             nc.vector.tensor_copy(
@@ -93,7 +91,8 @@ def tile_picked_ybeamfr_log_p_kernel(tc, x_words, x_scales, w1, w2, unit, w3, of
             for t0 in range(0, PACK, 2):
                 slots = slice(t0, t0 + 2)
                 cols = slice(t0 * P, (t0 + 2) * P)
-                nc.scalar.copy(
+                cast = nc.scalar.copy if (c, t0) == (0, 0) else nc.vector.tensor_copy
+                cast(
                     out=w_bf[c][:, slots, :, :].rearrange("p t m j -> p m j t"),
                     in_=raw[:].rearrange("p j (m t) -> p m j t", t=PACK)[:, :, :, slots],
                 )
@@ -105,8 +104,10 @@ def tile_picked_ybeamfr_log_p_kernel(tc, x_words, x_scales, w1, w2, unit, w3, of
         nc.vector.tensor_copy(out=got_w[:, 0:S].bitcast(U32), in_=xw_win[:].bitcast(U32).indirect(offs_t[:]))
         quantise_weight(0, w1_raw)
         quantise_weight(1, w2_raw)
-        w3_raw = keep.tile([P, PACK, N], F32, name="w1_raw")
-        unit_t = keep.tile([P, PACK], F32, name="xw_win", align_bytes=64)
+        x_s = keep.tile([P, RUN + 1, P], U8, name="w1_raw", align_bytes=64)
+        x_w = keep.tile([P, RUN + 1, P], I32, name="xs_win", align_bytes=64)
+        w3_raw = keep.tile([P, PACK, N], F32, name="xw_win", align_bytes=64)
+        unit_t = keep.tile([P, PACK], F32, name="w_bf0", align_bytes=64)
         nc.sync.dma_start(out=w3_raw[:], in_=w3.rearrange("(p j) n -> p j n", j=PACK))
         nc.sync.dma_start(out=unit_t[:], in_=unit.rearrange("(p t) o -> p (t o)", t=PACK))
 
@@ -142,10 +143,7 @@ def tile_picked_ybeamfr_log_p_kernel(tc, x_words, x_scales, w1, w2, unit, w3, of
                     rhs=got_w[:, entries].bitcast(FP8X4), rhs_scale=got_s[:, entries], start=True, stop=True,
                 )
                 by_member = bank[:].rearrange("i (v d) -> i d v", d=2)
-                if t == 0:
-                    nc.vector.tensor_copy(out=a[:, vs], in_=by_member[:, 0, :])
-                else:
-                    nc.scalar.copy(out=a[:, vs], in_=by_member[:, 0, :])
+                nc.scalar.copy(out=a[:, vs], in_=by_member[:, 0, :])
                 nc.scalar.activation(out=squares[:, :, vs], in_=by_member, func=ACT.Square)
                 banks.append(by_member)
             both = terms.tile([P, V], F32, name="both")

from contextlib import ExitStack

import concourse.mybir as mybir
from concourse.masks import make_identity

K, T, S, H, V, N = 512, 2048, 1024, 512, 512, 128
FLOPS = 2 * 2 * K * H * S + 2 * H * N * V

F32 = mybir.dt.float32
BF16 = mybir.dt.bfloat16
I32 = mybir.dt.int32
U32 = mybir.dt.uint32
U16 = mybir.dt.uint16
U8 = mybir.dt.uint8
FP8X4 = mybir.dt.float8_e4m3fn_x4
ALU = mybir.AluOpType
ACT = mybir.ActivationFunctionType

P = 128
PACK = 4
RUN = S // P
PAIRS = RUN // 2
CHUNK = 256
LIST_ROWS = 16
LAG = 2
SPARE = 32
PLAIN = 2
TURNED = PACK - PLAIN
HALF = S // 2


def tile_picked_ybeamfr_log_p_kernel(tc, x_words, x_scales, w1, w2, unit, w3, offs, s1, s2, out):
    nc = tc.nc
    with ExitStack() as ctx:
        keep = ctx.enter_context(tc.tile_pool(name="keep", bufs=1))
        terms = ctx.enter_context(tc.tile_pool(name="terms", bufs=4))
        small = ctx.enter_context(tc.tile_pool(name="small", bufs=4))
        prod = ctx.enter_context(tc.psum_pool(name="prod", bufs=6))
        sums = ctx.enter_context(tc.psum_pool(name="sums", bufs=1))

        offs_t = keep.tile([P, S // LIST_ROWS], U16, name="offs_t")
        s1_t = keep.tile([P, V // LIST_ROWS], U16, name="s1_t")
        s2_t = keep.tile([P, V // LIST_ROWS], U16, name="s2_t")
        xs_win = keep.tile([P, T], U8, name="xs_win", align_bytes=64)
        one = keep.tile([P, 1], F32, name="xw_win", align_bytes=64)
        nc.gpsimd.memset(one[:], 1.0)
        nc.vector.memset(xs_win[:, 0 : 3 * T // 4].bitcast(I32), 0)
        nc.gpsimd.memset(xs_win[:, 3 * T // 4 :].bitcast(I32), 0)
        fifth = keep.tile([P, 1], F32, name="w1_raw", align_bytes=64)
        nc.vector.tensor_scalar(out=fifth[:], in0=one[:], scalar1=0.2, scalar2=None, op0=ALU.mult)
        ln_fifth = keep.tile([P, 1], F32, name="ln_fifth")
        nc.scalar.activation(out=ln_fifth[:], in_=fifth[:], func=ACT.Ln)

        nc.sync.dma_start(offs_t[:], offs)
        nc.sync.dma_start(s2_t[:], s2)
        nc.sync.dma_start(s1_t[:], s1)
        for q in range(4):
            queue = nc.sync if q < 2 else nc.scalar
            queue.dma_start(out=xs_win[32 * q : 32 * q + 4, :].bitcast(I32), in_=x_scales[0, 4 * q : 4 * q + 4, :].bitcast(I32))
        xw_win = keep.tile([P, T], I32, name="xw_win", align_bytes=64)
        nc.sync.dma_start(out=xw_win[:], in_=x_words[0].rearrange("p n r -> p (n r)").bitcast(I32))
        w1_raw = keep.tile([P, PACK, H], F32, name="w1_raw", align_bytes=64)
        nc.sync.dma_start(out=w1_raw[:], in_=w1.rearrange("(p j) c -> p j c", j=PACK))

        den = [keep.tile([P, V + SPARE], F32, name=f"den{t}") for t in range(PACK)]
        num = [keep.tile([P, V + SPARE], F32, name=f"num{t}") for t in range(PACK)]

        ident = keep.tile([P, P], F32, name="ident")
        make_identity(nc, ident[:])
        firsts = [[keep.tile([P, V + 8], F32, name=f"firsts{t}{c}") for c in range(2)] for t in range(PLAIN)]
        for window in den + num + sum(firsts, []):
            nc.gpsimd.memset(window[:, V:], 0.0)

        got_s = keep.tile([P, S + RUN], U8, name="got_s", align_bytes=64)
        nc.vector.memset(got_s[:, S:].bitcast(I32), 0)
        got_w = keep.tile([P, S + RUN], I32, name="got_w", align_bytes=64)
        nc.vector.memset(got_w[:, S:], 0)

        def deal(dealt, got):
            nc.vector.tensor_copy(
                out=dealt[:, 0:RUN, :].rearrange("k (u m) p -> k u p m", u=2),
                in_=got[:, 0:S].rearrange("k (p u m) -> k u p m", u=2, m=RUN // 2),
            )
            nc.vector.tensor_copy(out=dealt[:, RUN, :], in_=got[:, RUN : S + RUN : RUN])

        w_bf = [keep.tile([P, PACK, P, PACK], BF16, name=f"w_bf{c}", align_bytes=64) for c in range(2)]
        w_w = [keep.tile([P, H], U32, name=f"w_w{c}", align_bytes=64) for c in range(2)]
        w_s = [keep.tile([P, H], U8, name=f"w_s{c}", align_bytes=64) for c in range(2)]

        def quantise_weight(c, raw):
            for t0 in range(0, PACK, 2):
                slots = slice(t0, t0 + 2)
                cols = slice(t0 * P, (t0 + 2) * P)
                cast = nc.scalar.copy if (c, t0) == (0, 0) else nc.vector.tensor_copy
                cast(
                    out=w_bf[c][:, slots, :, :].rearrange("p t m j -> p m j t"),
                    in_=raw[:].rearrange("p j (m t) -> p m j t", t=PACK)[:, :, :, slots],
                )
                nc.vector.quantize_mx(out=w_w[c][:, cols].bitcast(FP8X4), scales=w_s[c][:, cols], in_=w_bf[c][:, slots, :, :].rearrange("p t m j -> p (t m j)"))

        nc.vector.tensor_copy(out=got_s[:, 0:S], in_=xs_win[:].indirect(offs_t[:]))
        w2_raw = keep.tile([P, PACK, H], F32, name="xs_win", align_bytes=64)
        nc.sync.dma_start(out=w2_raw[:], in_=w2.rearrange("(p j) c -> p j c", j=PACK))
        nc.vector.tensor_copy(out=got_w[:, 0:S].bitcast(U32), in_=xw_win[:].bitcast(U32).indirect(offs_t[:]))
        quantise_weight(0, w1_raw)
        quantise_weight(1, w2_raw)
        x_s = keep.tile([P, RUN + 1, P], U8, name="w1_raw", align_bytes=64)
        x_w = keep.tile([P, RUN + 1, P], I32, name="xs_win", align_bytes=64)
        w3_raw = keep.tile([P, PACK, N], F32, name="xw_win", align_bytes=64)
        unit_t = keep.tile([P, PACK], F32, name="w_bf0", align_bytes=64)
        nc.sync.dma_start(out=w3_raw[:], in_=w3.rearrange("(p j) n -> p j n", j=PACK))
        nc.sync.dma_start(out=unit_t[:], in_=unit.rearrange("(p t) o -> p (t o)", t=PACK))

        def product(bank, m, c, cols):
            nc.tensor.matmul_mx(
                out=bank,
                lhsT=x_w[:, m, :].bitcast(FP8X4),
                lhsT_scale=x_s[:, m, :],
                rhs=w_w[c][:, cols].bitcast(FP8X4),
                rhs_scale=w_s[c][:, cols],
                start=True,
                stop=True,
            )

        even = [keep.tile([P, TURNED, PAIRS + 1, P], F32, name=f"even{c}") for c in range(2)]

        def last_even(c):
            bank = sums.tile([P, TURNED * P], F32, name=("power", "corr")[c])
            product(bank[:], RUN, c, slice(PLAIN * P, H))
            nc.scalar.copy(out=even[c][:, :, PAIRS, :], in_=bank[:].rearrange("v (t i) -> v t i", t=TURNED))

        def plain_terms(t, c):
            cols = slice(t * P, (t + 1) * P)
            a = firsts[t][c]
            squares = terms.tile([P, 2, V], F32, name="squares")
            banks = []
            for u in range(2):
                entries = slice(u * HALF, (u + 1) * HALF)
                vs = slice(u * CHUNK, (u + 1) * CHUNK)
                bank = prod.tile([P, HALF], F32, name="bank")
                nc.tensor.matmul_mx(
                    out=bank[:], lhsT=w_w[c][:, cols].bitcast(FP8X4), lhsT_scale=w_s[c][:, cols],
                    rhs=got_w[:, entries].bitcast(FP8X4), rhs_scale=got_s[:, entries], start=True, stop=True,
                )
                by_member = bank[:].rearrange("i (v d) -> i d v", d=2)
                nc.scalar.copy(out=a[:, vs], in_=by_member[:, 0, :])
                nc.scalar.activation(out=squares[:, :, vs], in_=by_member, func=ACT.Square)
                banks.append(by_member)
            both = terms.tile([P, V], F32, name="both")
            nc.vector.tensor_tensor(out=both[:], in0=a[:, 0:V], in1=a[:, 1 : V + 1], op=ALU.add)
            cross = terms.tile([P, V], F32, name="cross")
            for u in range(2):
                vs = slice(u * CHUNK, (u + 1) * CHUNK)
                nc.vector.tensor_tensor(out=cross[:, vs], in0=banks[u][:, 1, :], in1=both[:, vs], op=ALU.mult)
            return squares, cross

        def plain_windows(t, re_terms, im_terms):
            power = small.tile([P, 2, V], F32, name="power2")
            nc.vector.tensor_tensor(out=power[:], in0=re_terms[0][:], in1=im_terms[0][:], op=ALU.add)
            nc.vector.scalar_tensor_tensor(out=den[t][:, 0:V], in0=power[:, 0, :], scalar=0.9, in1=power[:, 1, :], op0=ALU.add, op1=ALU.add)
            partial = small.tile([P, V], F32, name="partial")
            nc.vector.scalar_tensor_tensor(out=partial[:], in0=re_terms[1][:], scalar=0.5, in1=den[t][:, 0:V], op0=ALU.add, op1=ALU.subtract)
            signed = small.tile([P, V], F32, name="signed")
            nc.vector.tensor_tensor(out=signed[:], in0=partial[:], in1=im_terms[1][:], op=ALU.add)
            nc.scalar.activation(out=num[t][:, 0:V], in_=signed[:], func=ACT.Abs, scale=5.0)

        def make_terms(t, c):
            cols = slice(t * P, (t + 1) * P)
            bank_a = prod.tile([P, PAIRS * P], F32, name="bank")
            for h in range(PAIRS):
                product(bank_a[:, h * P : (h + 1) * P], 2 * h, c, cols)
            bank_b = prod.tile([P, PAIRS * P], F32, name="bank")
            for h in range(PAIRS):
                product(bank_b[:, h * P : (h + 1) * P], 2 * h + 1, c, cols)
            a_all = even[c][:, t - PLAIN, :, :].rearrange("v h i -> v (h i)")
            a = a_all[:, 0 : PAIRS * P]
            nc.scalar.copy(out=a, in_=bank_a[:])
            sq_b = terms.tile([P, PAIRS * P], F32, name="sq_b")
            nc.scalar.activation(out=sq_b[:], in_=bank_b[:], func=ACT.Square)
            both = terms.tile([P, PAIRS * P], F32, name="both")
            nc.vector.tensor_tensor(out=both[:], in0=a, in1=a_all[:, P:], op=ALU.add)
            sq_a = terms.tile([P, PAIRS * P], F32, name="sq_a")
            nc.scalar.activation(out=sq_a[:], in_=a, func=ACT.Square)
            cross = terms.tile([P, PAIRS * P], F32, name="cross")
            nc.vector.tensor_tensor(out=cross[:], in0=bank_b[:], in1=both[:], op=ALU.mult)
            return sq_b, sq_a, cross

        def add_turned(bank, parts, first, last):
            for n, part in enumerate(parts):
                for h in range(PAIRS):
                    cols = slice(h * P, (h + 1) * P)
                    nc.tensor.matmul(
                        bank[:, cols], lhsT=part[:, cols], rhs=ident[:], is_transpose=True,
                        start=first and n == 0 and h == 0,
                        stop=last and n == len(parts) - 1 and h == PAIRS - 1,
                    )

        hid = keep.tile([P, PACK - 1, V], BF16, name="hid", align_bytes=64)
        woven = keep.tile([P, V, PACK], BF16, name="woven", align_bytes=64)

        def windows(t, re_terms, im_terms):
            power = sums.tile([P, V], F32, name="power")
            corr = sums.tile([P, V], F32, name="corr")
            add_turned(power, re_terms[:2], True, False)
            add_turned(corr, re_terms[2:], True, False)
            add_turned(power, im_terms[:2], False, True)
            add_turned(corr, im_terms[2:], False, True)
            den_v = den[t][:, 0:V].rearrange("i (p h) -> i p h", h=PAIRS)
            nc.vector.tensor_scalar(out=den_v, in0=power[:].rearrange("i (h p) -> i p h", h=PAIRS), scalar1=0.9, scalar2=None, op0=ALU.add)
            signed = small.tile([P, V], F32, name="signed")
            nc.vector.scalar_tensor_tensor(
                out=signed[:].rearrange("i (p h) -> i p h", h=PAIRS), in0=corr[:].rearrange("i (h p) -> i p h", h=PAIRS), scalar=0.5,
                in1=den_v, op0=ALU.add, op1=ALU.subtract,
            )
            nc.scalar.activation(out=num[t][:, 0:V], in_=signed[:], func=ACT.Abs, scale=5.0)

        def hidden(t, v0, width):
            lst = slice(v0 // LIST_ROWS, (v0 + width) // LIST_ROWS)
            cols = slice(v0, v0 + width)
            args = small.tile([P, 2, width], F32, name="args")
            nc.scalar.activation(out=args[:, 0, :], in_=den[t][:].indirect(s2_t[:, lst]), func=ACT.Copy)
            nc.vector.tensor_tensor(out=args[:, 1, :], in0=num[t][:].indirect(s1_t[:, lst]), in1=args[:, 0, :], op=ALU.add)
            logs = small.tile([P, 2, width], F32, name="logs")
            nc.scalar.activation(out=logs[:], in_=args[:], func=ACT.Ln)
            diff = small.tile([P, width], F32, name="diff")
            nc.vector.scalar_tensor_tensor(out=diff[:], in0=logs[:, 1, :], scalar=ln_fifth[:], in1=logs[:, 0, :], op0=ALU.add, op1=ALU.subtract)
            target = woven[:, cols, t] if t == PACK - 1 else hid[:, t, cols]
            nc.vector.tensor_scalar(out=target, in0=diff[:], scalar1=unit_t[:, t : t + 1], scalar2=None, op0=ALU.mult)
            if t == PACK - 2:
                nc.vector.tensor_copy(out=woven[:, cols, 0 : PACK - 1], in_=hid[:, :, cols].rearrange("p t v -> p v t"))

        w3_bf = keep.tile([P, N, PACK], BF16, name="w3_bf", align_bytes=64)
        w3_w = keep.tile([P, N], U32, name="w3_w", align_bytes=64)
        w3_s = keep.tile([P, N], U8, name="w3_s", align_bytes=64)

        def features(v0, width):
            hid_w = small.tile([P, width], U32, name="hid_w", align_bytes=64)
            hid_s = small.tile([P, width], U8, name="hid_s", align_bytes=64)
            nc.vector.quantize_mx(out=hid_w[:].bitcast(FP8X4), scales=hid_s[:], in_=woven[:, v0 : v0 + width, :].rearrange("p v t -> p (v t)"))
            bank = prod.tile([P, width], F32, name="bank")
            nc.tensor.matmul_mx(
                out=bank[:], lhsT=w3_w[:].bitcast(FP8X4), lhsT_scale=w3_s[:], rhs=hid_w[:].bitcast(FP8X4), rhs_scale=hid_s[:],
                start=True, stop=True,
            )
            result = small.tile([P, width], F32, name="result")
            nc.scalar.copy(out=result[:], in_=bank[:])
            nc.sync.dma_start(out=out[:, v0 : v0 + width], in_=result[:])

        for t in range(PACK):
            if t < PLAIN:
                plain_windows(t, plain_terms(t, 0), plain_terms(t, 1))
            else:
                if t == PLAIN:
                    deal(x_s[:], got_s[:])
                    deal(x_w[:].bitcast(U32), got_w[:].bitcast(U32))
                    last_even(0)
                    last_even(1)
                windows(t, make_terms(t, 0), make_terms(t, 1))
            if t >= LAG:
                hidden(t - LAG, 0, V)
        nc.scalar.copy(out=w3_bf[:], in_=w3_raw[:].rearrange("p j n -> p n j"))
        nc.vector.quantize_mx(out=w3_w[:].bitcast(FP8X4), scales=w3_s[:], in_=w3_bf[:].rearrange("p n j -> p (n j)"))
        for t in range(PACK - LAG, PACK - 1):
            hidden(t, 0, V)
        for v0 in range(0, V, CHUNK):
            hidden(PACK - 1, v0, CHUNK)
            features(v0, CHUNK)
